import numpy as np
import ml_dtypes


def mxq(x, axis, fmt="e4m3"):
    dtype, down = {"e4m3": (ml_dtypes.float8_e4m3fn, 7), "e5m2": (ml_dtypes.float8_e5m2, 14)}[fmt]
    v = np.moveaxis(np.asarray(x, np.float32).astype(ml_dtypes.bfloat16).astype(np.float64), axis, -1)
    blocks = v.reshape(v.shape[:-1] + (-1, 32))
    amax = np.abs(blocks).max(-1, keepdims=True)
    byte = np.maximum(np.where(amax > 0, np.frexp(amax)[1] - 1 + 127, 0) - down, 1)
    scale = np.exp2(byte - 127.0)
    codes = (blocks / scale).astype(np.float32).astype(dtype).astype(np.float64)
    return np.moveaxis((codes * scale).reshape(v.shape), -1, axis)


WIDE = False


def mx_kscale(k):
    if not WIDE:
        return np.ones(k)
    levels = np.array([10, -10, 5, -5, 0])
    if k % 512:
        return np.exp2(np.random.permutation(np.resize(levels, k // 32))).repeat(32)
    a = np.empty((k // 512, 16))
    for p in range(k // 512):
        a[p, :8] = np.random.permutation(np.resize(levels, 8))
        for g in range(8):
            far = levels[np.abs(levels - a[p, g]) >= 10]
            a[p, g + 8] = far[np.random.randint(len(far))]
    return np.exp2(a.ravel()).repeat(32)


def f64(x):
    return np.asarray(x).astype(np.float64)


def striped(idx):
    return np.tile(idx.reshape(-1, 16).T, (8, 1)).astype(np.uint16)


def unstriped(offs):
    return offs[:16].T.reshape(-1).astype(np.int64)

def planes(y):
    n, m = y.shape
    v = y.astype(np.float32).astype(ml_dtypes.bfloat16).astype(np.float64).reshape(n // 32, 32, m)
    top = np.abs(v).max(1)
    byte = np.clip(np.where(top > 0, np.frexp(top)[1] - 1 + 127 - 7, 1), 1, 254)
    codes = (v * np.exp2(127.0 - byte)[:, None, :]).reshape(n, m).astype(np.float32).astype(ml_dtypes.float8_e4m3fn).view(np.uint8)
    words = codes.reshape(n // 512, 128, 4, m).transpose(0, 1, 3, 2)
    return np.ascontiguousarray(words), np.ascontiguousarray(byte.astype(np.uint8).reshape(n // 512, 16, m))


K, T, S, V, N = 512, 1024, 512, 256, 512
P = 2 ** 7


def setup_inputs():
    n = np.random.standard_normal
    s = mx_kscale(K)[:, None]
    return {
        "xT": (n((K, T)) * s).astype(np.float32),
        "w1": (n((K, N)) / np.sqrt(K) / s).astype(np.float32),
        "fx": np.tile(np.random.uniform(0.05, 0.95, V), (P, 1)).astype(np.float32),
        "fy": np.tile(np.random.uniform(0.05, 0.95, V), (P, 1)).astype(np.float32),
        "offs": striped(np.random.permutation(T)[:S]),
        "c00": striped(np.random.permutation(S)[:V]),
        "c01": striped(np.random.permutation(S)[:V]),
        "c10": striped(np.random.permutation(S)[:V]),
        "c11": striped(np.random.permutation(S)[:V]),
    }


def reference(xT, w1, fx, fy, offs, c00, c01, c10, c11):
    xq = mxq(f64(xT)[:, unstriped(offs)], 0, "e4m3")
    y = mxq(f64(w1), 0, "e4m3").T @ xq
    top = y[:, unstriped(c00)] + (y[:, unstriped(c01)] - y[:, unstriped(c00)]) * f64(fx)[:1]
    low = y[:, unstriped(c10)] + (y[:, unstriped(c11)] - y[:, unstriped(c10)]) * f64(fx)[:1]
    out_0 = top + (low - top) * f64(fy)[:1]
    return (out_0,) + planes(out_0)

@@ -1,0 +1,199 @@
+from contextlib import ExitStack
+
+import concourse.mybir as mybir
+from concourse.masks import make_identity
+
+K, T, S, V, N = 512, 1024, 512, 256, 512
+FLOPS = 2 * K * S * N
+
+F32 = mybir.dt.float32
+BF16 = mybir.dt.bfloat16
+U32 = mybir.dt.uint32
+I32 = mybir.dt.int32
+U16 = mybir.dt.uint16
+U8 = mybir.dt.uint8
+FP8X4 = mybir.dt.float8_e4m3fn_x4
+MULT = mybir.AluOpType.mult
+ADD = mybir.AluOpType.add
+
+P = 128
+PACK = 4
+HALF_S = S // 2
+HALF_V = V // 2
+
+
+def tile_picked_bilin_none_lo_kernel(
+    tc, xT, w1, fx, fy, offs, c00, c01, c10, c11, out_0, out_1, out_2
+):
+    nc = tc.nc
+    with ExitStack() as ctx:
+        sb = ctx.enter_context(tc.tile_pool(name="sb", bufs=1))
+        ps = ctx.enter_context(tc.psum_pool(name="ps", bufs=1))
+
+        def tile(name, shape, dtype):
+            return sb.tile(shape, dtype, name=name, align_bytes=64)
+
+        def bank(number, shape):
+            return ps.tile(shape, F32, name="bank%d" % number)
+
+        x_rows = xT.rearrange("(p j) c -> p j c", j=PACK)
+        w_rows = w1.rearrange("(p j) c -> p j c", j=PACK)
+        x_plane = [tile("x_plane%d" % j, [P, T], F32) for j in range(PACK)]
+        w_half = [tile("w_half%d" % h, [P, PACK, N // 2], F32) for h in range(2)]
+        picked = sb.tile([P, S // 16], U16, name="picked")
+        corner = [sb.tile([P, V // 16], U16, name="corner%d" % c) for c in range(4)]
+        fx_col = tile("fx_col", [P, 2], F32)
+        fy_col = tile("fy_col", [P, 2], F32)
+
+        nc.scalar.dma_start(out=fx_col[:], in_=fx[0:1, :].rearrange("o (p e) -> (o p) e", e=2))
+        nc.scalar.dma_start(out=fy_col[:], in_=fy[0:1, :].rearrange("o (p e) -> (o p) e", e=2))
+        nc.sync.dma_start(out=x_plane[0][:], in_=x_rows[:, 0, :])
+        nc.sync.dma_start(picked[:], offs)
+        for j in range(1, PACK):
+            nc.sync.dma_start(out=x_plane[j][:], in_=x_rows[:, j, :])
+        for h in range(2):
+            nc.sync.dma_start(out=w_half[h][:], in_=w_rows[:, :, h * (N // 2) : (h + 1) * (N // 2)])
+        for c, lst in enumerate((c00, c01, c10, c11)):
+            nc.sync.dma_start(corner[c][:], lst)
+
+        ident = tile("ident", [P, P], F32)
+        make_identity(nc, ident[:])
+
+        gx_col = tile("gx_col", [P, 2], F32)
+        gy_col = tile("gy_col", [P, 2], F32)
+        nc.vector.tensor_scalar(out=gx_col[:], in0=fx_col[:], scalar1=-1.0, scalar2=1.0, op0=MULT, op1=ADD)
+        nc.vector.tensor_scalar(out=gy_col[:], in0=fy_col[:], scalar1=-1.0, scalar2=1.0, op0=MULT, op1=ADD)
+        weight_col = tile("weight_col", [P, 4, 2], F32)
+        for c, (a, b) in enumerate(((gx_col, gy_col), (fx_col, gy_col), (gx_col, fy_col), (fx_col, fy_col))):
+            nc.vector.tensor_tensor(weight_col[:, c, :], a[:], b[:], MULT)
+        weight_row = []
+        for u in range(2):
+            spread = bank(6 + u, [P, 2, 2, P])
+            for i in range(2):
+                for e in range(2):
+                    nc.tensor.transpose(
+                        spread[:, i, e, :], weight_col[:, 2 * u + i, e : e + 1].to_broadcast([P, P]), ident[:]
+                    )
+            rows = tile("weight_rows%d" % u, [P, 2, V], F32)
+            nc.scalar.copy(
+                out=rows[:].rearrange("p i (n e) -> p i n e", e=2), in_=spread[:].rearrange("p i e n -> p i n e")
+            )
+            weight_row.extend([rows[:, 0, :], rows[:, 1, :]])
+
+        x_pair = [tile("x_pair%d" % u, [P, 2, S], F32) for u in range(2)]
+        for j in range(PACK):
+            nc.vector.tensor_copy(x_pair[j // 2][:, j % 2, :], x_plane[j][:].indirect(picked[:]))
+        x_bf = [tile("x_bf%d" % h, [P, HALF_S, PACK], BF16) for h in range(2)]
+        x_codes = tile("x_codes", [P, S], U32)
+        x_scales = tile("x_scales", [P, S], U8)
+        for h in range(2):
+            cols = slice(h * HALF_S, (h + 1) * HALF_S)
+            nc.scalar.copy(out=x_bf[h][:, :, 0:2], in_=x_pair[0][:, :, cols].rearrange("p j s -> p s j"))
+        for h in range(2):
+            cols = slice(h * HALF_S, (h + 1) * HALF_S)
+            nc.vector.tensor_copy(out=x_bf[h][:, :, 2:4], in_=x_pair[1][:, :, cols].rearrange("p j s -> p s j"))
+        for h in range(2):
+            cols = slice(h * HALF_S, (h + 1) * HALF_S)
+            nc.vector.quantize_mx(
+                out=x_codes[:, cols].bitcast(FP8X4),
+                scales=x_scales[:, cols],
+                in_=x_bf[h][:].rearrange("p s j -> p (s j)"),
+            )
+
+        w_bf = [tile("w_bf%d" % u, [P, 2, P, PACK], BF16) for u in range(2)]
+        w_codes = [tile("w_codes%d" % t, [P, P], U32) for t in range(PACK)]
+        w_scales = [tile("w_scales%d" % t, [P, P], U8) for t in range(PACK)]
+        y = [tile("y%d" % t, [P, S], F32) for t in range(PACK)]
+
+        def product(acc, t, cols):
+            nc.tensor.matmul_mx(
+                out=acc,
+                lhsT=w_codes[t][:].bitcast(FP8X4),
+                lhsT_scale=w_scales[t][:],
+                rhs=x_codes[:, cols].bitcast(FP8X4),
+                rhs_scale=x_scales[:, cols],
+                start=True,
+                stop=True,
+            )
+            nc.scalar.copy(out=y[t][:, cols], in_=acc)
+
+        for u in range(2):
+            for h in range(2):
+                nc.scalar.copy(
+                    out=w_bf[u][:, :, h * 64 : (h + 1) * 64, :].rearrange("p t m j -> p m t j"),
+                    in_=w_half[h][:].rearrange("p j (m t) -> p m t j", t=PACK)[:, :, 2 * u : 2 * u + 2, :],
+                )
+            for t in (2 * u, 2 * u + 1):
+                nc.vector.quantize_mx(
+                    out=w_codes[t][:].bitcast(FP8X4),
+                    scales=w_scales[t][:],
+                    in_=w_bf[u][:, t % 2, :, :].rearrange("p m j -> p (m j)"),
+                )
+                if t == 0:
+                    for h in range(2):
+                        product(bank(h, [P, HALF_S])[:], t, slice(h * HALF_S, (h + 1) * HALF_S))
+                else:
+                    product(bank(1 + t, [P, S])[:], t, slice(0, S))
+
+        out_rows = out_0.rearrange("(p t) v -> p t v", t=PACK)
+        result = [tile("result%d" % u, [P, 2, V], F32) for u in range(2)]
+        o_bf = [tile("o_bf%d" % h, [P, HALF_V, PACK], BF16) for h in range(2)]
+        for t in range(PACK):
+            terms = [tile("term%d_%d" % (t, c), [P, V], F32) for c in range(4)]
+            res = result[t // 2][:, t % 2, :]
+            if t < PACK - 1:
+                banks = (5, 6, 7) if t % 2 == 0 else (0, 1, 2)
+                turned = [bank(banks[h], [P, P]) for h in range(2)]
+                for c in range(4):
+                    nc.vector.tensor_tensor(terms[c][:], y[t][:].indirect(corner[c][:]), weight_row[c], MULT)
+                    for h in range(2):
+                        nc.tensor.matmul(
+                            turned[h][:],
+                            lhsT=terms[c][:, h * HALF_V : (h + 1) * HALF_V],
+                            rhs=ident[:],
+                            is_transpose=True,
+                            start=(c == 0),
+                            stop=(c == 3),
+                        )
+                back = bank(banks[2], [P, V])
+                for h in range(2):
+                    turned_sb = tile("turned_sb%d_%d" % (t, h), [P, P], F32)
+                    nc.scalar.copy(out=turned_sb[:], in_=turned[h][:])
+                    nc.tensor.transpose(back[:, h * HALF_V : (h + 1) * HALF_V], turned_sb[:], ident[:])
+                nc.scalar.copy(out=res, in_=back[:])
+            else:
+                upper = tile("upper", [P, V], F32)
+                three = tile("three", [P, V], F32)
+                for c in range(4):
+                    nc.vector.tensor_tensor(terms[c][:], y[t][:].indirect(corner[c][:]), weight_row[c], MULT)
+                    if c == 2:
+                        nc.vector.tensor_tensor(upper[:], terms[0][:], terms[1][:], ADD)
+                nc.vector.tensor_tensor(three[:], upper[:], terms[2][:], ADD)
+                nc.vector.tensor_tensor(res, three[:], terms[3][:], ADD)
+            nc.sync.dma_start(out=out_rows[:, t, :], in_=res)
+            if t == 1:
+                for h in range(2):
+                    cols = slice(h * HALF_V, (h + 1) * HALF_V)
+                    nc.scalar.copy(out=o_bf[h][:, :, 0:2], in_=result[0][:, :, cols].rearrange("p t v -> p v t"))
+
+        o_codes = tile("o_codes", [P, V], U32)
+        o_scales = tile("o_scales", [P, V], U8)
+        for h in range(2):
+            cols = slice(h * HALF_V, (h + 1) * HALF_V)
+            nc.vector.tensor_copy(out=o_bf[h][:, :, 2:4], in_=result[1][:, :, cols].rearrange("p t v -> p v t"))
+        for h in range(2):
+            cols = slice(h * HALF_V, (h + 1) * HALF_V)
+            nc.vector.quantize_mx(
+                out=o_codes[:, cols].bitcast(FP8X4),
+                scales=o_scales[:, cols],
+                in_=o_bf[h][:].rearrange("p v t -> p (v t)"),
+            )
+        nc.sync.dma_start(
+            out=out_1[0].rearrange("l c r -> l (c r)").bitcast(I32), in_=o_codes[:].bitcast(I32)
+        )
+        scale_rows = out_2[0].bitcast(I32)
+        for q in range(4):
+            queue = nc.scalar if q % 2 == 0 else nc.sync
+            queue.dma_start(
+                out=scale_rows[4 * q : 4 * q + 4, :], in_=o_scales[32 * q : 32 * q + 4, :].bitcast(I32)
+            )

@@ -15,6 +15,7 @@ U8 = mybir.dt.uint8
 FP8X4 = mybir.dt.float8_e4m3fn_x4
 MULT = mybir.AluOpType.mult
 ADD = mybir.AluOpType.add
+COPY = mybir.ActivationFunctionType.Copy
 
 P = 128
 PACK = 4
@@ -39,7 +40,8 @@ def tile_picked_bilin_none_lo_kernel(
         x_rows = xT.rearrange("(p j) c -> p j c", j=PACK)
         w_rows = w1.rearrange("(p j) c -> p j c", j=PACK)
         x_plane = [tile("x_plane%d" % j, [P, T], F32) for j in range(PACK)]
-        w_half = [tile("w_half%d" % h, [P, PACK, N // 2], F32) for h in range(2)]
+        w_pieces = ((0, 0, N), (1, 0, N // 2), (1, N // 2, N))
+        w_raw = [tile("w_raw%d" % i, [P, 2, hi - lo], F32) for i, (u, lo, hi) in enumerate(w_pieces)]
         picked = sb.tile([P, S // 16], U16, name="picked")
         corner = [sb.tile([P, V // 16], U16, name="corner%d" % c) for c in range(4)]
         fx_col = tile("fx_col", [P, 2], F32)
@@ -51,57 +53,68 @@ def tile_picked_bilin_none_lo_kernel(
         nc.sync.dma_start(picked[:], offs)
         for j in range(1, PACK):
             nc.sync.dma_start(out=x_plane[j][:], in_=x_rows[:, j, :])
-        for h in range(2):
-            nc.sync.dma_start(out=w_half[h][:], in_=w_rows[:, :, h * (N // 2) : (h + 1) * (N // 2)])
+        for raw, (u, lo, hi) in zip(w_raw, w_pieces):
+            nc.sync.dma_start(out=raw[:], in_=w_rows[:, 2 * u : 2 * u + 2, lo:hi])
         for c, lst in enumerate((c00, c01, c10, c11)):
             nc.sync.dma_start(corner[c][:], lst)
 
         ident = tile("ident", [P, P], F32)
         make_identity(nc, ident[:])
 
-        gx_col = tile("gx_col", [P, 2], F32)
+        x_side = tile("x_side", [P, 2, 2], F32)
         gy_col = tile("gy_col", [P, 2], F32)
-        nc.vector.tensor_scalar(out=gx_col[:], in0=fx_col[:], scalar1=-1.0, scalar2=1.0, op0=MULT, op1=ADD)
-        nc.vector.tensor_scalar(out=gy_col[:], in0=fy_col[:], scalar1=-1.0, scalar2=1.0, op0=MULT, op1=ADD)
-        weight_col = tile("weight_col", [P, 4, 2], F32)
-        for c, (a, b) in enumerate(((gx_col, gy_col), (fx_col, gy_col), (gx_col, fy_col), (fx_col, fy_col))):
-            nc.vector.tensor_tensor(weight_col[:, c, :], a[:], b[:], MULT)
-        weight_row = []
-        for u in range(2):
-            spread = bank(6 + u, [P, 2, 2, P])
+        nc.scalar.activation(x_side[:, 0, :], fx_col[:], COPY, bias=1.0, scale=-1.0)
+        nc.scalar.copy(out=x_side[:, 1, :], in_=fx_col[:])
+        nc.scalar.activation(gy_col[:], fy_col[:], COPY, bias=1.0, scale=-1.0)
+        spread = []
+        for u, y_side in enumerate((gy_col, fy_col)):
+            weight_col = tile(("weight_col", "x_bf")[u], [P, 2, 2], F32)
+            for e in range(2):
+                nc.scalar.activation(weight_col[:, :, e], x_side[:, :, e], COPY, scale=y_side[:, e : e + 1])
+            spread.append(bank(6 + u, [P, 2, 2, P]))
             for i in range(2):
                 for e in range(2):
                     nc.tensor.transpose(
-                        spread[:, i, e, :], weight_col[:, 2 * u + i, e : e + 1].to_broadcast([P, P]), ident[:]
+                        spread[u][:, i, e, :], weight_col[:, i, e : e + 1].to_broadcast([P, P]), ident[:]
                     )
-            rows = tile("weight_rows%d" % u, [P, 2, V], F32)
-            nc.scalar.copy(
-                out=rows[:].rearrange("p i (n e) -> p i n e", e=2), in_=spread[:].rearrange("p i e n -> p i n e")
-            )
-            weight_row.extend([rows[:, 0, :], rows[:, 1, :]])
 
-        x_pair = [tile("x_pair%d" % u, [P, 2, S], F32) for u in range(2)]
-        for j in range(PACK):
-            nc.vector.tensor_copy(x_pair[j // 2][:, j % 2, :], x_plane[j][:].indirect(picked[:]))
-        x_bf = [tile("x_bf%d" % h, [P, HALF_S, PACK], BF16) for h in range(2)]
+        def spread_rows(u, name):
+            rows = tile(name, [P, 2, V], F32)
+            nc.scalar.copy(
+                out=rows[:].rearrange("p i (n e) -> p i n e", e=2), in_=spread[u][:].rearrange("p i e n -> p i n e")
+            )
+            return [rows[:, 0, :], rows[:, 1, :]]
+
+
+        weight_row = spread_rows(0, "weight_rows0") + spread_rows(1, "weight_rows1")
+
+        x_bf = tile("x_bf", [P, S, PACK], BF16)
         x_codes = tile("x_codes", [P, S], U32)
         x_scales = tile("x_scales", [P, S], U8)
+        pair = [tile("pair%d" % h, [P, 2, HALF_S], BF16) for h in range(2)]
+        picked_half = [picked[:, h * (HALF_S // 16) : (h + 1) * (HALF_S // 16)] for h in range(2)]
+        for j in range(2):
+            for h in range(2):
+                nc.vector.tensor_copy(pair[h][:, j, :], x_plane[j][:].indirect(picked_half[h]))
         for h in range(2):
-            cols = slice(h * HALF_S, (h + 1) * HALF_S)
-            nc.scalar.copy(out=x_bf[h][:, :, 0:2], in_=x_pair[0][:, :, cols].rearrange("p j s -> p s j"))
+            nc.scalar.copy(
+                out=x_bf[:, h * HALF_S : (h + 1) * HALF_S, 0:2], in_=pair[h][:].rearrange("p j s -> p s j")
+            )
+        nc.vector.tensor_copy(x_bf[:, :, 2], x_plane[2][:].indirect(picked[:]))
         for h in range(2):
-            cols = slice(h * HALF_S, (h + 1) * HALF_S)
-            nc.vector.tensor_copy(out=x_bf[h][:, :, 2:4], in_=x_pair[1][:, :, cols].rearrange("p j s -> p s j"))
+            nc.vector.tensor_copy(
+                x_bf[:, h * HALF_S : (h + 1) * HALF_S, 3],
+                x_plane[3][:].indirect(picked_half[h]),
+            )
         for h in range(2):
             cols = slice(h * HALF_S, (h + 1) * HALF_S)
             nc.vector.quantize_mx(
                 out=x_codes[:, cols].bitcast(FP8X4),
                 scales=x_scales[:, cols],
-                in_=x_bf[h][:].rearrange("p s j -> p (s j)"),
+                in_=x_bf[:, cols, :].rearrange("p s j -> p (s j)"),
             )
 
-        w_bf = [tile("w_bf%d" % u, [P, 2, P, PACK], BF16) for u in range(2)]
-        w_codes = [tile("w_codes%d" % t, [P, P], U32) for t in range(PACK)]
+        w_codes = [tile(name, [P, P], U32) for name in ("x_bf", "w_codes1", "w_codes2", "w_codes3")]
         w_scales = [tile("w_scales%d" % t, [P, P], U8) for t in range(PACK)]
         y = [tile("y%d" % t, [P, S], F32) for t in range(PACK)]
 
@@ -115,31 +128,45 @@ def tile_picked_bilin_none_lo_kernel(
                 start=True,
                 stop=True,
             )
-            nc.scalar.copy(out=y[t][:, cols], in_=acc)
 
-        for u in range(2):
-            for h in range(2):
-                nc.scalar.copy(
-                    out=w_bf[u][:, :, h * 64 : (h + 1) * 64, :].rearrange("p t m j -> p m t j"),
-                    in_=w_half[h][:].rearrange("p j (m t) -> p m t j", t=PACK)[:, :, 2 * u : 2 * u + 2, :],
+        def deal(copy, dealt, tiles):
+            for raw, (u, lo, hi) in zip(w_raw, w_pieces):
+                copy(
+                    out=dealt[:, :, lo // PACK : hi // PACK, 2 * u : 2 * u + 2].rearrange("p t m j -> p m t j"),
+                    in_=raw[:].rearrange("p j (m t) -> p m t j", t=PACK)[:, :, tiles, :],
                 )
-            for t in (2 * u, 2 * u + 1):
-                nc.vector.quantize_mx(
-                    out=w_codes[t][:].bitcast(FP8X4),
-                    scales=w_scales[t][:],
-                    in_=w_bf[u][:, t % 2, :, :].rearrange("p m j -> p (m j)"),
-                )
-                if t == 0:
-                    for h in range(2):
-                        product(bank(h, [P, HALF_S])[:], t, slice(h * HALF_S, (h + 1) * HALF_S))
-                else:
-                    product(bank(1 + t, [P, S])[:], t, slice(0, S))
+
+        def quantize_weights(dealt, first, t):
+            nc.vector.quantize_mx(
+                out=w_codes[t][:].bitcast(FP8X4),
+                scales=w_scales[t][:],
+                in_=dealt[:, t - first, :, :].rearrange("p m j -> p (m j)"),
+            )
+
+        early = [tile("pair%d" % t, [P, 1, P, PACK], BF16) for t in range(2)]
+        for t in range(2):
+            deal(nc.scalar.copy, early[t], slice(t, t + 1))
+        quantize_weights(early[0], 0, 0)
+        late = tile("pair0", [P, 2, P, PACK], BF16)
+        deal(nc.vector.tensor_copy, late, slice(2, 4))
+        quantize_weights(early[1], 1, 1)
+        for t in (2, 3):
+            quantize_weights(late, 2, t)
+        for i, number in enumerate((0, 1, 5, 6)):
+            cols = slice(i * P, (i + 1) * P)
+            acc = bank(number, [P, P])
+            product(acc[:], 0, cols)
+            nc.scalar.copy(out=y[0][:, cols], in_=acc[:])
+        for t in range(1, PACK):
+            acc = bank(1 + t, [P, S])
+            product(acc[:], t, slice(0, S))
+            nc.scalar.copy(out=y[t][:], in_=acc[:])
 
         out_rows = out_0.rearrange("(p t) v -> p t v", t=PACK)
         result = [tile("result%d" % u, [P, 2, V], F32) for u in range(2)]
         o_bf = [tile("o_bf%d" % h, [P, HALF_V, PACK], BF16) for h in range(2)]
         for t in range(PACK):
-            terms = [tile("term%d_%d" % (t, c), [P, V], F32) for c in range(4)]
+            terms = [tile("pair0" if (t, c) == (0, 1) else "term%d_%d" % (t, c), [P, V], F32) for c in range(4)]
             res = result[t // 2][:, t % 2, :]
             if t < PACK - 1:
                 banks = (5, 6, 7) if t % 2 == 0 else (0, 1, 2)
@@ -168,8 +195,12 @@ def tile_picked_bilin_none_lo_kernel(
                     nc.vector.tensor_tensor(terms[c][:], y[t][:].indirect(corner[c][:]), weight_row[c], MULT)
                     if c == 2:
                         nc.vector.tensor_tensor(upper[:], terms[0][:], terms[1][:], ADD)
-                nc.vector.tensor_tensor(three[:], upper[:], terms[2][:], ADD)
-                nc.vector.tensor_tensor(res, three[:], terms[3][:], ADD)
+                for h in range(2):
+                    cols = slice(h * HALF_V, (h + 1) * HALF_V)
+                    nc.vector.tensor_tensor(three[:, cols], upper[:, cols], terms[2][:, cols], ADD)
+                for h in range(2):
+                    cols = slice(h * HALF_V, (h + 1) * HALF_V)
+                    nc.vector.tensor_tensor(result[1][:, 1, cols], three[:, cols], terms[3][:, cols], ADD)
             nc.sync.dma_start(out=out_rows[:, t, :], in_=res)
             if t == 1:
                 for h in range(2):
@@ -178,6 +209,7 @@ def tile_picked_bilin_none_lo_kernel(
 
         o_codes = tile("o_codes", [P, V], U32)
         o_scales = tile("o_scales", [P, V], U8)
+        word_rows = out_1[0].rearrange("l c r -> l (c r)").bitcast(I32)
         for h in range(2):
             cols = slice(h * HALF_V, (h + 1) * HALF_V)
             nc.vector.tensor_copy(out=o_bf[h][:, :, 2:4], in_=result[1][:, :, cols].rearrange("p t v -> p v t"))
@@ -188,9 +220,7 @@ def tile_picked_bilin_none_lo_kernel(
                 scales=o_scales[:, cols],
                 in_=o_bf[h][:].rearrange("p v t -> p (v t)"),
             )
-        nc.sync.dma_start(
-            out=out_1[0].rearrange("l c r -> l (c r)").bitcast(I32), in_=o_codes[:].bitcast(I32)
-        )
+            nc.sync.dma_start(out=word_rows[:, cols], in_=o_codes[:, cols].bitcast(I32))
         scale_rows = out_2[0].bitcast(I32)
         for q in range(4):
             queue = nc.scalar if q % 2 == 0 else nc.sync

@@ -40,21 +40,21 @@ def tile_picked_bilin_none_lo_kernel(
         x_rows = xT.rearrange("(p j) c -> p j c", j=PACK)
         w_rows = w1.rearrange("(p j) c -> p j c", j=PACK)
         x_plane = [tile("x_plane%d" % j, [P, T], F32) for j in range(PACK)]
-        w_pieces = ((0, 0, N), (1, 0, N // 2), (1, N // 2, N))
-        w_raw = [tile("w_raw%d" % i, [P, 2, hi - lo], F32) for i, (u, lo, hi) in enumerate(w_pieces)]
+        w_raw = [tile("w_raw%d" % u, [P, PACK, N // 2], F32) for u in range(2)]
         picked = sb.tile([P, S // 16], U16, name="picked")
         corner = [sb.tile([P, V // 16], U16, name="corner%d" % c) for c in range(4)]
         fx_col = tile("fx_col", [P, 2], F32)
         fy_col = tile("fy_col", [P, 2], F32)
 
-        nc.scalar.dma_start(out=fx_col[:], in_=fx[0:1, :].rearrange("o (p e) -> (o p) e", e=2))
-        nc.scalar.dma_start(out=fy_col[:], in_=fy[0:1, :].rearrange("o (p e) -> (o p) e", e=2))
         nc.sync.dma_start(out=x_plane[0][:], in_=x_rows[:, 0, :])
         nc.sync.dma_start(picked[:], offs)
         for j in range(1, PACK):
             nc.sync.dma_start(out=x_plane[j][:], in_=x_rows[:, j, :])
-        for raw, (u, lo, hi) in zip(w_raw, w_pieces):
-            nc.sync.dma_start(out=raw[:], in_=w_rows[:, 2 * u : 2 * u + 2, lo:hi])
+            if j == 1:
+                nc.sync.dma_start(out=fx_col[:], in_=fx[0:1, :].rearrange("o (p e) -> (o p) e", e=2))
+                nc.sync.dma_start(out=fy_col[:], in_=fy[0:1, :].rearrange("o (p e) -> (o p) e", e=2))
+        for u in range(2):
+            nc.sync.dma_start(out=w_raw[u][:], in_=w_rows[:, :, u * (N // 2) : (u + 1) * (N // 2)])
         for c, lst in enumerate((c00, c01, c10, c11)):
             nc.sync.dma_start(corner[c][:], lst)
 
@@ -66,161 +66,170 @@ def tile_picked_bilin_none_lo_kernel(
         nc.scalar.activation(x_side[:, 0, :], fx_col[:], COPY, bias=1.0, scale=-1.0)
         nc.scalar.copy(out=x_side[:, 1, :], in_=fx_col[:])
         nc.scalar.activation(gy_col[:], fy_col[:], COPY, bias=1.0, scale=-1.0)
-        spread = []
+        weight_row = []
         for u, y_side in enumerate((gy_col, fy_col)):
             weight_col = tile(("weight_col", "x_bf")[u], [P, 2, 2], F32)
             for e in range(2):
                 nc.scalar.activation(weight_col[:, :, e], x_side[:, :, e], COPY, scale=y_side[:, e : e + 1])
-            spread.append(bank(6 + u, [P, 2, 2, P]))
+            spread = bank(6 + u, [P, 2, 2, P])
             for i in range(2):
                 for e in range(2):
-                    nc.tensor.transpose(
-                        spread[u][:, i, e, :], weight_col[:, i, e : e + 1].to_broadcast([P, P]), ident[:]
-                    )
-
-        def spread_rows(u, name):
-            rows = tile(name, [P, 2, V], F32)
+                    nc.tensor.transpose(spread[:, i, e, :], weight_col[:, i, e : e + 1].to_broadcast([P, P]), ident[:])
+            rows = tile("weight_rows%d" % u, [P, 2, V], F32)
             nc.scalar.copy(
-                out=rows[:].rearrange("p i (n e) -> p i n e", e=2), in_=spread[u][:].rearrange("p i e n -> p i n e")
+                out=rows[:].rearrange("p i (n e) -> p i n e", e=2), in_=spread[:].rearrange("p i e n -> p i n e")
             )
-            return [rows[:, 0, :], rows[:, 1, :]]
+            weight_row.extend([rows[:, 0, :], rows[:, 1, :]])
 
-
-        weight_row = spread_rows(0, "weight_rows0") + spread_rows(1, "weight_rows1")
-
-        x_bf = tile("x_bf", [P, S, PACK], BF16)
         x_codes = tile("x_codes", [P, S], U32)
         x_scales = tile("x_scales", [P, S], U8)
-        pair = [tile("pair%d" % h, [P, 2, HALF_S], BF16) for h in range(2)]
-        picked_half = [picked[:, h * (HALF_S // 16) : (h + 1) * (HALF_S // 16)] for h in range(2)]
-        for j in range(2):
-            for h in range(2):
-                nc.vector.tensor_copy(pair[h][:, j, :], x_plane[j][:].indirect(picked_half[h]))
-        for h in range(2):
-            nc.scalar.copy(
-                out=x_bf[:, h * HALF_S : (h + 1) * HALF_S, 0:2], in_=pair[h][:].rearrange("p j s -> p s j")
-            )
-        nc.vector.tensor_copy(x_bf[:, :, 2], x_plane[2][:].indirect(picked[:]))
+        pairs = tile("pairs", [P, 2, 2, HALF_S, 2], BF16)
+        for j in range(PACK - 1):
+            nc.vector.tensor_copy(pairs[:, :, j // 2, :, j % 2], x_plane[j][:].indirect(picked[:]))
         for h in range(2):
             nc.vector.tensor_copy(
-                x_bf[:, h * HALF_S : (h + 1) * HALF_S, 3],
-                x_plane[3][:].indirect(picked_half[h]),
+                pairs[:, h, 1, :, 1],
+                x_plane[3][:].indirect(picked[:, h * (HALF_S // 16) : (h + 1) * (HALF_S // 16)]),
             )
-        for h in range(2):
-            cols = slice(h * HALF_S, (h + 1) * HALF_S)
-            nc.vector.quantize_mx(
-                out=x_codes[:, cols].bitcast(FP8X4),
-                scales=x_scales[:, cols],
-                in_=x_bf[:, cols, :].rearrange("p s j -> p (s j)"),
+        pieces = ((0, HALF_S), (HALF_S, HALF_S + P), (HALF_S + P, S))
+        x_bf = tile("x_bf", [P, S * PACK], BF16)
+        for lo, hi in pieces:
+            words = pairs[:, lo // HALF_S, :, :, :].rearrange("p u s e -> p (u s e)").bitcast(U32)
+            nc.scalar.copy(
+                out=x_bf[:, lo * PACK : hi * PACK].bitcast(U32).rearrange("p (c i u) -> p c u i", i=2, u=2),
+                in_=words.rearrange("p (u c i) -> p c u i", u=2, i=2)[:, lo % HALF_S // 2 : (lo % HALF_S + hi - lo) // 2, :, :],
             )
 
-        w_codes = [tile(name, [P, P], U32) for name in ("x_bf", "w_codes1", "w_codes2", "w_codes3")]
-        w_scales = [tile("w_scales%d" % t, [P, P], U8) for t in range(PACK)]
-        y = [tile("y%d" % t, [P, S], F32) for t in range(PACK)]
+        def quantize(codes, scales, values):
+            nc.vector.quantize_mx(out=codes.bitcast(FP8X4), scales=scales, in_=values)
 
-        def product(acc, t, cols):
+        def quantize_x(i):
+            lo, hi = pieces[i]
+            quantize(x_codes[:, lo:hi], x_scales[:, lo:hi], x_bf[:, lo * PACK : hi * PACK])
+
+        def product(acc, codes, scales, cols):
             nc.tensor.matmul_mx(
                 out=acc,
-                lhsT=w_codes[t][:].bitcast(FP8X4),
-                lhsT_scale=w_scales[t][:],
+                lhsT=codes.bitcast(FP8X4),
+                lhsT_scale=scales,
                 rhs=x_codes[:, cols].bitcast(FP8X4),
                 rhs_scale=x_scales[:, cols],
                 start=True,
                 stop=True,
             )
 
-        def deal(copy, dealt, tiles):
-            for raw, (u, lo, hi) in zip(w_raw, w_pieces):
-                copy(
-                    out=dealt[:, :, lo // PACK : hi // PACK, 2 * u : 2 * u + 2].rearrange("p t m j -> p m t j"),
-                    in_=raw[:].rearrange("p j (m t) -> p m t j", t=PACK)[:, :, tiles, :],
-                )
+        w_view = [raw[:].rearrange("p j (m t) -> p m j t", t=PACK) for raw in w_raw]
+        y = [tile("y0", [P, S], F32)]
+        low_codes = [tile("low_codes%d" % u, [P, P], U32) for u in range(2)]
+        low_scales = [tile("low_scales%d" % u, [P, P], U8) for u in range(2)]
 
-        def quantize_weights(dealt, first, t):
-            nc.vector.quantize_mx(
-                out=w_codes[t][:].bitcast(FP8X4),
-                scales=w_scales[t][:],
-                in_=dealt[:, t - first, :, :].rearrange("p m j -> p (m j)"),
+        def deal_low(u, name):
+            dealt = tile(name, [P, P // 2, 2, PACK], BF16)
+            nc.vector.tensor_copy(
+                out=dealt[:].rearrange("p m t j -> p m j t"), in_=w_view[u][:, :, :, 0:2]
             )
+            return dealt[:].rearrange("p m t j -> p (m t j)")
 
-        early = [tile("pair%d" % t, [P, 1, P, PACK], BF16) for t in range(2)]
+        dealt = deal_low(0, "x_plane2")
+        quantize_x(0)
+        quantize(low_codes[0][:], low_scales[0][:], dealt)
+        quantize_x(1)
+        quantize_x(2)
+        dealt_late = tile("pairs", [P, 3, P * PACK], BF16)
+        dealt_high = dealt_late[:, 1:3, :].rearrange("p t (u m j) -> p u m j t", u=2, j=PACK)
+        nc.scalar.copy(out=dealt_high[:, 0, :, :, :], in_=w_view[0][:, :, :, 2:4])
+        for i, (lo, hi) in enumerate(pieces):
+            acc = bank(i, [P, hi - lo])
+            product(acc[:], low_codes[0][:], low_scales[0][:], slice(lo, hi))
+            nc.scalar.copy(out=y[0][:, lo:hi], in_=acc[:])
+        nc.vector.tensor_copy(
+            out=dealt_late[:, 0, :].rearrange("p (m t j) -> p m j t", t=2, j=PACK), in_=w_view[1][:, :, :, 0:2]
+        )
+        nc.vector.tensor_copy(out=dealt_high[:, 1, :, :, :], in_=w_view[1][:, :, :, 2:4])
+        quantize(low_codes[1][:], low_scales[1][:], dealt_late[:, 0, :])
+        high_codes = tile("high_codes", [P, 2 * P], U32)
+        high_scales = tile("high_scales", [P, 2 * P], U8)
+        quantize(high_codes[:], high_scales[:], dealt_late[:, 1:3, :].rearrange("p t n -> p (t n)"))
+        y.extend([tile(name, [P, S], F32) for name in ("y1", "y2", "y3")])
+        acc = bank(3, [P, S])
+        product(acc[:], low_codes[1][:], low_scales[1][:], slice(0, S))
+        nc.scalar.copy(out=y[1][:], in_=acc[:])
         for t in range(2):
-            deal(nc.scalar.copy, early[t], slice(t, t + 1))
-        quantize_weights(early[0], 0, 0)
-        late = tile("pair0", [P, 2, P, PACK], BF16)
-        deal(nc.vector.tensor_copy, late, slice(2, 4))
-        quantize_weights(early[1], 1, 1)
-        for t in (2, 3):
-            quantize_weights(late, 2, t)
-        for i, number in enumerate((0, 1, 5, 6)):
-            cols = slice(i * P, (i + 1) * P)
-            acc = bank(number, [P, P])
-            product(acc[:], 0, cols)
-            nc.scalar.copy(out=y[0][:, cols], in_=acc[:])
-        for t in range(1, PACK):
-            acc = bank(1 + t, [P, S])
-            product(acc[:], t, slice(0, S))
-            nc.scalar.copy(out=y[t][:], in_=acc[:])
+            acc = bank(4 + t, [P, S])
+            product(acc[:], high_codes[:, t * P : (t + 1) * P], high_scales[:, t * P : (t + 1) * P], slice(0, S))
+            nc.scalar.copy(out=y[2 + t][:], in_=acc[:])
 
-        out_rows = out_0.rearrange("(p t) v -> p t v", t=PACK)
-        result = [tile("result%d" % u, [P, 2, V], F32) for u in range(2)]
-        o_bf = [tile("o_bf%d" % h, [P, HALF_V, PACK], BF16) for h in range(2)]
-        for t in range(PACK):
-            terms = [tile("pair0" if (t, c) == (0, 1) else "term%d_%d" % (t, c), [P, V], F32) for c in range(4)]
-            res = result[t // 2][:, t % 2, :]
-            if t < PACK - 1:
-                banks = (5, 6, 7) if t % 2 == 0 else (0, 1, 2)
-                turned = [bank(banks[h], [P, P]) for h in range(2)]
-                for c in range(4):
-                    nc.vector.tensor_tensor(terms[c][:], y[t][:].indirect(corner[c][:]), weight_row[c], MULT)
-                    for h in range(2):
-                        nc.tensor.matmul(
-                            turned[h][:],
-                            lhsT=terms[c][:, h * HALF_V : (h + 1) * HALF_V],
-                            rhs=ident[:],
-                            is_transpose=True,
-                            start=(c == 0),
-                            stop=(c == 3),
-                        )
-                back = bank(banks[2], [P, V])
-                for h in range(2):
-                    turned_sb = tile("turned_sb%d_%d" % (t, h), [P, P], F32)
-                    nc.scalar.copy(out=turned_sb[:], in_=turned[h][:])
-                    nc.tensor.transpose(back[:, h * HALF_V : (h + 1) * HALF_V], turned_sb[:], ident[:])
-                nc.scalar.copy(out=res, in_=back[:])
+        halves = [slice(h * HALF_V, (h + 1) * HALF_V) for h in range(2)]
+
+        later_terms = []
+
+        def weighted(t, c):
+            if c == 0:
+                term = tile("term_first%d" % t, [P, V], F32)[:]
             else:
-                upper = tile("upper", [P, V], F32)
-                three = tile("three", [P, V], F32)
-                for c in range(4):
-                    nc.vector.tensor_tensor(terms[c][:], y[t][:].indirect(corner[c][:]), weight_row[c], MULT)
-                    if c == 2:
-                        nc.vector.tensor_tensor(upper[:], terms[0][:], terms[1][:], ADD)
+                if c == 1:
+                    later_terms.append(tile("terms%d" % t, [P, 3, V], F32))
+                term = later_terms[t][:, c - 1, :]
+            nc.vector.tensor_tensor(term, y[t][:].indirect(corner[c][:]), weight_row[c], MULT)
+            return term
+
+        def add_turned(turned, term, c, last):
+            nc.tensor.matmul(turned, lhsT=term, rhs=ident[:], is_transpose=True, start=(c == 0), stop=(c == last))
+
+        out_flat = out_0.rearrange("(p t) v -> p (t v)", t=PACK)
+        o_bf = [tile("o_bf%d" % h, [P, HALF_V, PACK], BF16) for h in range(2)]
+
+        low_turned = [tile("low_turned%d" % h, [P, 2, P], F32) for h in range(2)]
+        for u in range(2):
+            turned = [bank((6, 4)[u] + h, [P, P]) for h in range(2)]
+            for c in range(4):
+                term = weighted(u, c)
                 for h in range(2):
-                    cols = slice(h * HALF_V, (h + 1) * HALF_V)
-                    nc.vector.tensor_tensor(three[:, cols], upper[:, cols], terms[2][:, cols], ADD)
+                    add_turned(turned[h][:], term[:, halves[h]], c, 3)
+            for h in range(2):
+                nc.scalar.copy(
+                    out=low_turned[h][:, :, u * (P // 2) : (u + 1) * (P // 2)],
+                    in_=turned[h][:].rearrange("v (m t) -> v t m", t=2),
+                )
+        low_back = bank(0, [P, 2, V])
+        for t in range(2):
+            for h in range(2):
+                nc.tensor.transpose(low_back[:, t, halves[h]], low_turned[h][:, t, :], ident[:])
+        low_result = tile("low_result", [P, 2, V], F32)
+        nc.scalar.copy(out=low_result[:], in_=low_back[:])
+        nc.sync.dma_start(out=out_flat[:, 0 : 2 * V], in_=low_result[:].rearrange("p t v -> p (t v)"))
+        for h in range(2):
+            nc.scalar.copy(out=o_bf[h][:, :, 0:2], in_=low_result[:, :, halves[h]].rearrange("p t v -> p v t"))
+
+        high_back = []
+        for t in (2, 3):
+            turned = [bank((2, 6)[t - 2] + h, [P, P]) for h in range(2)]
+            for c in range(3):
+                term = weighted(t, c)
                 for h in range(2):
-                    cols = slice(h * HALF_V, (h + 1) * HALF_V)
-                    nc.vector.tensor_tensor(result[1][:, 1, cols], three[:, cols], terms[3][:, cols], ADD)
-            nc.sync.dma_start(out=out_rows[:, t, :], in_=res)
-            if t == 1:
-                for h in range(2):
-                    cols = slice(h * HALF_V, (h + 1) * HALF_V)
-                    nc.scalar.copy(out=o_bf[h][:, :, 0:2], in_=result[0][:, :, cols].rearrange("p t v -> p v t"))
+                    add_turned(turned[h][:], term[:, halves[h]], c, 2)
+            back = bank((1, 4)[t - 2], [P, V])
+            for h in range(2):
+                turned_sb = tile("turned%d_%d" % (t, h), [P, P], F32)
+                nc.scalar.copy(out=turned_sb[:], in_=turned[h][:])
+                nc.tensor.transpose(back[:, halves[h]], turned_sb[:], ident[:])
+            high_back.append(back)
+        last = [weighted(t, 3) for t in (2, 3)]
+        high_result = tile("high_result", [P, 2, V], F32)
+        nc.vector.tensor_tensor(high_result[:, 0, :], last[0], high_back[0][:], ADD)
+        nc.sync.dma_start(out=out_flat[:, 2 * V : 3 * V], in_=high_result[:, 0, :])
+        for h in range(2):
+            nc.vector.tensor_tensor(high_result[:, 1, halves[h]], last[1][:, halves[h]], high_back[1][:, halves[h]], ADD)
+        nc.sync.dma_start(out=out_flat[:, 3 * V :], in_=high_result[:, 1, :])
 
         o_codes = tile("o_codes", [P, V], U32)
         o_scales = tile("o_scales", [P, V], U8)
         word_rows = out_1[0].rearrange("l c r -> l (c r)").bitcast(I32)
         for h in range(2):
-            cols = slice(h * HALF_V, (h + 1) * HALF_V)
-            nc.vector.tensor_copy(out=o_bf[h][:, :, 2:4], in_=result[1][:, :, cols].rearrange("p t v -> p v t"))
+            nc.vector.tensor_copy(out=o_bf[h][:, :, 2:4], in_=high_result[:, :, halves[h]].rearrange("p t v -> p v t"))
         for h in range(2):
-            cols = slice(h * HALF_V, (h + 1) * HALF_V)
-            nc.vector.quantize_mx(
-                out=o_codes[:, cols].bitcast(FP8X4),
-                scales=o_scales[:, cols],
-                in_=o_bf[h][:].rearrange("p v t -> p (v t)"),
-            )
-            nc.sync.dma_start(out=word_rows[:, cols], in_=o_codes[:, cols].bitcast(I32))
+            quantize(o_codes[:, halves[h]], o_scales[:, halves[h]], o_bf[h][:].rearrange("p v t -> p (v t)"))
+            nc.sync.dma_start(out=word_rows[:, halves[h]], in_=o_codes[:, halves[h]].bitcast(I32))
         scale_rows = out_2[0].bitcast(I32)
         for q in range(4):
             queue = nc.scalar if q % 2 == 0 else nc.sync

@@ -43,16 +43,15 @@ def tile_picked_bilin_none_lo_kernel(
         w_raw = [tile("w_raw%d" % u, [P, PACK, N // 2], F32) for u in range(2)]
         picked = sb.tile([P, S // 16], U16, name="picked")
         corner = [sb.tile([P, V // 16], U16, name="corner%d" % c) for c in range(4)]
-        fx_col = tile("fx_col", [P, 2], F32)
-        fy_col = tile("fy_col", [P, 2], F32)
+        f_rows = tile("f_rows", [P, P], F32)
+        nc.vector.memset(f_rows[:], 0.0)
 
         nc.sync.dma_start(out=x_plane[0][:], in_=x_rows[:, 0, :])
         nc.sync.dma_start(picked[:], offs)
+        for a, f in enumerate((fx, fy)):
+            nc.sync.dma_start(out=f_rows[2 * a : 2 * a + 2, :], in_=f[0:1, :].rearrange("o (h n) -> (o h) n", h=2))
         for j in range(1, PACK):
             nc.sync.dma_start(out=x_plane[j][:], in_=x_rows[:, j, :])
-            if j == 1:
-                nc.sync.dma_start(out=fx_col[:], in_=fx[0:1, :].rearrange("o (p e) -> (o p) e", e=2))
-                nc.sync.dma_start(out=fy_col[:], in_=fy[0:1, :].rearrange("o (p e) -> (o p) e", e=2))
         for u in range(2):
             nc.sync.dma_start(out=w_raw[u][:], in_=w_rows[:, :, u * (N // 2) : (u + 1) * (N // 2)])
         for c, lst in enumerate((c00, c01, c10, c11)):
@@ -61,24 +60,22 @@ def tile_picked_bilin_none_lo_kernel(
         ident = tile("ident", [P, P], F32)
         make_identity(nc, ident[:])
 
-        x_side = tile("x_side", [P, 2, 2], F32)
-        gy_col = tile("gy_col", [P, 2], F32)
-        nc.scalar.activation(x_side[:, 0, :], fx_col[:], COPY, bias=1.0, scale=-1.0)
-        nc.scalar.copy(out=x_side[:, 1, :], in_=fx_col[:])
-        nc.scalar.activation(gy_col[:], fy_col[:], COPY, bias=1.0, scale=-1.0)
+        f_turned = bank(5, [P, P])
+        nc.tensor.transpose(f_turned[:], f_rows[:], ident[:])
+        sides = tile("sides", [P, 2, 4], F32)
+        nc.scalar.activation(sides[:, 0, :], f_turned[:, 0:4], COPY, bias=1.0, scale=-1.0)
+        nc.scalar.copy(out=sides[:, 1, :], in_=f_turned[:, 0:4])
         weight_row = []
-        for u, y_side in enumerate((gy_col, fy_col)):
+        for u in range(2):
             weight_col = tile(("weight_col", "x_bf")[u], [P, 2, 2], F32)
-            for e in range(2):
-                nc.scalar.activation(weight_col[:, :, e], x_side[:, :, e], COPY, scale=y_side[:, e : e + 1])
+            for h in range(2):
+                nc.scalar.activation(weight_col[:, :, h], sides[:, :, h], COPY, scale=sides[:, u, 2 + h : 3 + h])
             spread = bank(6 + u, [P, 2, 2, P])
             for i in range(2):
-                for e in range(2):
-                    nc.tensor.transpose(spread[:, i, e, :], weight_col[:, i, e : e + 1].to_broadcast([P, P]), ident[:])
+                for h in range(2):
+                    nc.tensor.transpose(spread[:, i, h, :], weight_col[:, i, h : h + 1].to_broadcast([P, P]), ident[:])
             rows = tile("weight_rows%d" % u, [P, 2, V], F32)
-            nc.scalar.copy(
-                out=rows[:].rearrange("p i (n e) -> p i n e", e=2), in_=spread[:].rearrange("p i e n -> p i n e")
-            )
+            nc.scalar.copy(out=rows[:].rearrange("p i v -> p (i v)"), in_=spread[:].rearrange("p i h n -> p (i h n)"))
             weight_row.extend([rows[:, 0, :], rows[:, 1, :]])
 
         x_codes = tile("x_codes", [P, S], U32)
@@ -208,18 +205,23 @@ def tile_picked_bilin_none_lo_kernel(
                 term = weighted(t, c)
                 for h in range(2):
                     add_turned(turned[h][:], term[:, halves[h]], c, 2)
-            back = bank((1, 4)[t - 2], [P, V])
+            if t == 2:
+                whole = bank(1, [P, V])
+                back = [whole[:, halves[h]] for h in range(2)]
+                high_back.append(whole[:])
+            else:
+                back = [bank(4 + h, [P, P])[:] for h in range(2)]
+                high_back.append(back)
             for h in range(2):
                 turned_sb = tile("turned%d_%d" % (t, h), [P, P], F32)
                 nc.scalar.copy(out=turned_sb[:], in_=turned[h][:])
-                nc.tensor.transpose(back[:, halves[h]], turned_sb[:], ident[:])
-            high_back.append(back)
+                nc.tensor.transpose(back[h], turned_sb[:], ident[:])
         last = [weighted(t, 3) for t in (2, 3)]
         high_result = tile("high_result", [P, 2, V], F32)
-        nc.vector.tensor_tensor(high_result[:, 0, :], last[0], high_back[0][:], ADD)
+        nc.vector.tensor_tensor(high_result[:, 0, :], last[0], high_back[0], ADD)
         nc.sync.dma_start(out=out_flat[:, 2 * V : 3 * V], in_=high_result[:, 0, :])
         for h in range(2):
-            nc.vector.tensor_tensor(high_result[:, 1, halves[h]], last[1][:, halves[h]], high_back[1][:, halves[h]], ADD)
+            nc.vector.tensor_tensor(high_result[:, 1, halves[h]], last[1][:, halves[h]], high_back[1][h], ADD)
         nc.sync.dma_start(out=out_flat[:, 3 * V :], in_=high_result[:, 1, :])
 
         o_codes = tile("o_codes", [P, V], U32)

@@ -67,7 +67,7 @@ def tile_picked_bilin_none_lo_kernel(
         nc.scalar.copy(out=sides[:, 1, :], in_=f_turned[:, 0:4])
         weight_row = []
         for u in range(2):
-            weight_col = tile(("weight_col", "x_bf")[u], [P, 2, 2], F32)
+            weight_col = tile(("pairs", "x_bf")[u], [P, 2, 2], F32)
             for h in range(2):
                 nc.scalar.activation(weight_col[:, :, h], sides[:, :, h], COPY, scale=sides[:, u, 2 + h : 3 + h])
             spread = bank(6 + u, [P, 2, 2, P])
@@ -81,8 +81,11 @@ def tile_picked_bilin_none_lo_kernel(
         x_codes = tile("x_codes", [P, S], U32)
         x_scales = tile("x_scales", [P, S], U8)
         pairs = tile("pairs", [P, 2, 2, HALF_S, 2], BF16)
-        for j in range(PACK - 1):
-            nc.vector.tensor_copy(pairs[:, :, j // 2, :, j % 2], x_plane[j][:].indirect(picked[:]))
+        first_rows = tile("first_rows", [P, 2, S], BF16)
+        for j in range(2):
+            nc.vector.tensor_copy(first_rows[:, j, :], x_plane[j][:].indirect(picked[:]))
+        nc.scalar.copy(out=pairs[:, :, 0, :, :], in_=first_rows[:].rearrange("p e (h s) -> p h s e", h=2))
+        nc.vector.tensor_copy(pairs[:, :, 1, :, 0], x_plane[2][:].indirect(picked[:]))
         for h in range(2):
             nc.vector.tensor_copy(
                 pairs[:, h, 1, :, 1],
@@ -92,9 +95,10 @@ def tile_picked_bilin_none_lo_kernel(
         x_bf = tile("x_bf", [P, S * PACK], BF16)
         for lo, hi in pieces:
             words = pairs[:, lo // HALF_S, :, :, :].rearrange("p u s e -> p (u s e)").bitcast(U32)
+            first = lo % HALF_S // 2
             nc.scalar.copy(
                 out=x_bf[:, lo * PACK : hi * PACK].bitcast(U32).rearrange("p (c i u) -> p c u i", i=2, u=2),
-                in_=words.rearrange("p (u c i) -> p c u i", u=2, i=2)[:, lo % HALF_S // 2 : (lo % HALF_S + hi - lo) // 2, :, :],
+                in_=words.rearrange("p (u c i) -> p c u i", u=2, i=2)[:, first : first + (hi - lo) // 2, :, :],
             )
 
         def quantize(codes, scales, values):
@@ -120,18 +124,13 @@ def tile_picked_bilin_none_lo_kernel(
         low_codes = [tile("low_codes%d" % u, [P, P], U32) for u in range(2)]
         low_scales = [tile("low_scales%d" % u, [P, P], U8) for u in range(2)]
 
-        def deal_low(u, name):
-            dealt = tile(name, [P, P // 2, 2, PACK], BF16)
-            nc.vector.tensor_copy(
-                out=dealt[:].rearrange("p m t j -> p m j t"), in_=w_view[u][:, :, :, 0:2]
-            )
-            return dealt[:].rearrange("p m t j -> p (m t j)")
-
-        dealt = deal_low(0, "x_plane2")
+        dealt_first = tile("x_plane2", [P, P // 2, 2, PACK], BF16)
+        nc.vector.tensor_copy(out=dealt_first[:].rearrange("p m t j -> p m j t"), in_=w_view[0][:, :, :, 0:2])
         quantize_x(0)
-        quantize(low_codes[0][:], low_scales[0][:], dealt)
+        quantize(low_codes[0][:], low_scales[0][:], dealt_first[:].rearrange("p m t j -> p (m t j)"))
         quantize_x(1)
         quantize_x(2)
+
         dealt_late = tile("pairs", [P, 3, P * PACK], BF16)
         dealt_high = dealt_late[:, 1:3, :].rearrange("p t (u m j) -> p u m j t", u=2, j=PACK)
         nc.scalar.copy(out=dealt_high[:, 0, :, :, :], in_=w_view[0][:, :, :, 2:4])
@@ -157,7 +156,6 @@ def tile_picked_bilin_none_lo_kernel(
             nc.scalar.copy(out=y[2 + t][:], in_=acc[:])
 
         halves = [slice(h * HALF_V, (h + 1) * HALF_V) for h in range(2)]
-
         later_terms = []
 
         def weighted(t, c):

@@ -131,23 +131,27 @@ def tile_picked_bilin_none_lo_kernel(
         quantize_x(1)
         quantize_x(2)
 
-        dealt_late = tile("pairs", [P, 3, P * PACK], BF16)
-        dealt_high = dealt_late[:, 1:3, :].rearrange("p t (u m j) -> p u m j t", u=2, j=PACK)
-        nc.scalar.copy(out=dealt_high[:, 0, :, :, :], in_=w_view[0][:, :, :, 2:4])
-        for i, (lo, hi) in enumerate(pieces):
+        dealt_scalar = tile("first_rows", [P, 2, P // 2, PACK], BF16)
+        nc.scalar.copy(out=dealt_scalar[:].rearrange("p t m j -> p m j t"), in_=w_view[0][:, :, :, 2:4])
+        for i, (lo, hi) in enumerate((lo, lo + P) for lo in range(0, S, P)):
             acc = bank(i, [P, hi - lo])
             product(acc[:], low_codes[0][:], low_scales[0][:], slice(lo, hi))
             nc.scalar.copy(out=y[0][:, lo:hi], in_=acc[:])
+        dealt_vector = tile("pairs", [P, 2, P * PACK], BF16)
+        dealt_high = dealt_vector[:, 1, :].rearrange("p (t m j) -> p t m j", t=2, j=PACK)
         nc.vector.tensor_copy(
-            out=dealt_late[:, 0, :].rearrange("p (m t j) -> p m j t", t=2, j=PACK), in_=w_view[1][:, :, :, 0:2]
+            out=dealt_vector[:, 0, :].rearrange("p (m t j) -> p m j t", t=2, j=PACK), in_=w_view[1][:, :, :, 0:2]
         )
-        nc.vector.tensor_copy(out=dealt_high[:, 1, :, :, :], in_=w_view[1][:, :, :, 2:4])
-        quantize(low_codes[1][:], low_scales[1][:], dealt_late[:, 0, :])
+        nc.vector.tensor_copy(out=dealt_high.rearrange("p t m j -> p m j t"), in_=w_view[1][:, :, :, 2:4])
+        quantize(low_codes[1][:], low_scales[1][:], dealt_vector[:, 0, :])
         high_codes = tile("high_codes", [P, 2 * P], U32)
         high_scales = tile("high_scales", [P, 2 * P], U8)
-        quantize(high_codes[:], high_scales[:], dealt_late[:, 1:3, :].rearrange("p t n -> p (t n)"))
+        for u, dealt in enumerate((dealt_scalar[:], dealt_high)):
+            for t in range(2):
+                cols = slice(t * P + u * (P // 2), t * P + (u + 1) * (P // 2))
+                quantize(high_codes[:, cols], high_scales[:, cols], dealt[:, t, :, :].rearrange("p m j -> p (m j)"))
         y.extend([tile(name, [P, S], F32) for name in ("y1", "y2", "y3")])
-        acc = bank(3, [P, S])
+        acc = bank(7, [P, S])
         product(acc[:], low_codes[1][:], low_scales[1][:], slice(0, S))
         nc.scalar.copy(out=y[1][:], in_=acc[:])
         for t in range(2):

@@ -66,10 +66,12 @@ def tile_picked_bilin_none_lo_kernel(
         nc.scalar.activation(sides[:, 0, :], f_turned[:, 0:4], COPY, bias=1.0, scale=-1.0)
         nc.scalar.copy(out=sides[:, 1, :], in_=f_turned[:, 0:4])
         weight_row = []
+        weight_keep = tile("weight_keep", [P, 4, 2], F32)
         for u in range(2):
             weight_col = tile(("pairs", "x_bf")[u], [P, 2, 2], F32)
             for h in range(2):
                 nc.scalar.activation(weight_col[:, :, h], sides[:, :, h], COPY, scale=sides[:, u, 2 + h : 3 + h])
+            nc.scalar.copy(out=weight_keep[:, 2 * u : 2 * u + 2, :], in_=weight_col[:])
             spread = bank(6 + u, [P, 2, 2, P])
             for i in range(2):
                 for h in range(2):
@@ -151,79 +153,94 @@ def tile_picked_bilin_none_lo_kernel(
                 cols = slice(t * P + u * (P // 2), t * P + (u + 1) * (P // 2))
                 quantize(high_codes[:, cols], high_scales[:, cols], dealt[:, t, :, :].rearrange("p m j -> p (m j)"))
         y.extend([tile(name, [P, S], F32) for name in ("y1", "y2", "y3")])
-        acc = bank(7, [P, S])
-        product(acc[:], low_codes[1][:], low_scales[1][:], slice(0, S))
-        nc.scalar.copy(out=y[1][:], in_=acc[:])
-        for t in range(2):
-            acc = bank(4 + t, [P, S])
-            product(acc[:], high_codes[:, t * P : (t + 1) * P], high_scales[:, t * P : (t + 1) * P], slice(0, S))
-            nc.scalar.copy(out=y[2 + t][:], in_=acc[:])
+
+        def project(t):
+            acc = bank((None, 7, 4, 5)[t], [P, S])
+            if t == 1:
+                product(acc[:], low_codes[1][:], low_scales[1][:], slice(0, S))
+            else:
+                cols = slice((t - 2) * P, (t - 1) * P)
+                product(acc[:], high_codes[:, cols], high_scales[:, cols], slice(0, S))
+            nc.scalar.copy(out=y[t][:], in_=acc[:])
 
         halves = [slice(h * HALF_V, (h + 1) * HALF_V) for h in range(2)]
-        later_terms = []
 
         def weighted(t, c):
-            if c == 0:
-                term = tile("term_first%d" % t, [P, V], F32)[:]
-            else:
-                if c == 1:
-                    later_terms.append(tile("terms%d" % t, [P, 3, V], F32))
-                term = later_terms[t][:, c - 1, :]
-            nc.vector.tensor_tensor(term, y[t][:].indirect(corner[c][:]), weight_row[c], MULT)
+            term = tile("term%d_%d" % (t, c), [P, V], F32)
+            nc.vector.tensor_tensor(term[:], y[t][:].indirect(corner[c][:]), weight_row[c], MULT)
             return term
 
-        def add_turned(turned, term, c, last):
-            nc.tensor.matmul(turned, lhsT=term, rhs=ident[:], is_transpose=True, start=(c == 0), stop=(c == last))
+        def plain(t, c):
+            term = tile("term%d_%d" % (t, c), [P, V], F32)
+            nc.scalar.activation(term[:], y[t][:].indirect(corner[c][:]), COPY)
+            return term
+
+        def turn(out, in_, start, stop):
+            nc.tensor.matmul(out, lhsT=in_, rhs=ident[:], is_transpose=True, start=start, stop=stop)
+
+        def add_turned(turned, term, first, last):
+            for h in range(2):
+                turn(turned[:, h, :], term[:, halves[h]], first and h == 0, last and h == 1)
 
         out_flat = out_0.rearrange("(p t) v -> p (t v)", t=PACK)
         o_bf = [tile("o_bf%d" % h, [P, HALF_V, PACK], BF16) for h in range(2)]
+        low_turned = tile("low_turned", [P, 2, 2, P], F32)
 
-        low_turned = [tile("low_turned%d" % h, [P, 2, P], F32) for h in range(2)]
-        for u in range(2):
-            turned = [bank((6, 4)[u] + h, [P, P]) for h in range(2)]
+        def low_sum(u, number):
+            turned = bank(number, [P, 2, P])
             for c in range(4):
-                term = weighted(u, c)
-                for h in range(2):
-                    add_turned(turned[h][:], term[:, halves[h]], c, 3)
+                add_turned(turned, weighted(u, c), c == 0, c == 3)
+            return turned
+
+        def low_copy(u, turned):
+            nc.scalar.copy(
+                out=low_turned[:, :, :, u * (P // 2) : (u + 1) * (P // 2)],
+                in_=turned[:].rearrange("v h (m t) -> v h t m", t=2),
+            )
+
+        project(1)
+        project(2)
+        turned0 = low_sum(0, 6)
+        spokes = [bank(c, [P, 2, P]) for c in range(3)]
+        for c in range(3):
+            add_turned(spokes[c], plain(2, c), True, True)
+            if c == 1:
+                low_copy(0, turned0)
+        project(3)
+        turned1 = low_sum(1, 3)
+        back = [bank(4, [P, V]), bank(5, [P, V])]
+        for c in range(3):
+            if c == 2:
+                low_copy(1, turned1)
+            scaled = tile("scaled%d" % c, [P, 2, P], F32)
             for h in range(2):
-                nc.scalar.copy(
-                    out=low_turned[h][:, :, u * (P // 2) : (u + 1) * (P // 2)],
-                    in_=turned[h][:].rearrange("v (m t) -> v t m", t=2),
-                )
-        low_back = bank(0, [P, 2, V])
+                nc.scalar.activation(scaled[:, h, :], spokes[c][:, h, :], COPY, scale=weight_keep[:, c, h : h + 1])
+                turn(back[0][:, halves[h]], scaled[:, h, :], c == 0 and h == 0, c == 2 and h == 1)
+        low_back = bank(7, [P, 2, V])
         for t in range(2):
             for h in range(2):
-                nc.tensor.transpose(low_back[:, t, halves[h]], low_turned[h][:, t, :], ident[:])
+                nc.tensor.transpose(low_back[:, t, halves[h]], low_turned[:, h, t, :], ident[:])
         low_result = tile("low_result", [P, 2, V], F32)
         nc.scalar.copy(out=low_result[:], in_=low_back[:])
         nc.sync.dma_start(out=out_flat[:, 0 : 2 * V], in_=low_result[:].rearrange("p t v -> p (t v)"))
+        turned3 = bank(6, [P, 2, P])
+        for c in range(2):
+            add_turned(turned3, weighted(3, c), c == 0, c == 1)
+        turned_sb = tile("turned3", [P, 2, P], F32)
+        nc.scalar.copy(out=turned_sb[:], in_=turned3[:])
+        for h in range(2):
+            turn(back[1][:, halves[h]], turned_sb[:, h, :], h == 0, h == 1)
         for h in range(2):
             nc.scalar.copy(out=o_bf[h][:, :, 0:2], in_=low_result[:, :, halves[h]].rearrange("p t v -> p v t"))
-
-        high_back = []
-        for t in (2, 3):
-            turned = [bank((2, 6)[t - 2] + h, [P, P]) for h in range(2)]
-            for c in range(3):
-                term = weighted(t, c)
-                for h in range(2):
-                    add_turned(turned[h][:], term[:, halves[h]], c, 2)
-            if t == 2:
-                whole = bank(1, [P, V])
-                back = [whole[:, halves[h]] for h in range(2)]
-                high_back.append(whole[:])
-            else:
-                back = [bank(4 + h, [P, P])[:] for h in range(2)]
-                high_back.append(back)
-            for h in range(2):
-                turned_sb = tile("turned%d_%d" % (t, h), [P, P], F32)
-                nc.scalar.copy(out=turned_sb[:], in_=turned[h][:])
-                nc.tensor.transpose(back[h], turned_sb[:], ident[:])
-        last = [weighted(t, 3) for t in (2, 3)]
         high_result = tile("high_result", [P, 2, V], F32)
-        nc.vector.tensor_tensor(high_result[:, 0, :], last[0], high_back[0], ADD)
+        last3 = [weighted(3, c) for c in (2, 3)]
+        last2 = weighted(2, 3)
+        pair3 = tile("pair3", [P, V], F32)
+        nc.vector.tensor_tensor(pair3[:], last3[0][:], last3[1][:], ADD)
+        nc.vector.tensor_tensor(high_result[:, 0, :], last2[:], back[0][:], ADD)
         nc.sync.dma_start(out=out_flat[:, 2 * V : 3 * V], in_=high_result[:, 0, :])
         for h in range(2):
-            nc.vector.tensor_tensor(high_result[:, 1, halves[h]], last[1][:, halves[h]], high_back[1][h], ADD)
+            nc.vector.tensor_tensor(high_result[:, 1, halves[h]], pair3[:, halves[h]], back[1][:, halves[h]], ADD)
         nc.sync.dma_start(out=out_flat[:, 3 * V :], in_=high_result[:, 1, :])
 
         o_codes = tile("o_codes", [P, V], U32)

@@ -216,13 +216,6 @@ def tile_picked_bilin_none_lo_kernel(
             for h in range(2):
                 nc.scalar.activation(scaled[:, h, :], spokes[c][:, h, :], COPY, scale=weight_keep[:, c, h : h + 1])
                 turn(back[0][:, halves[h]], scaled[:, h, :], c == 0 and h == 0, c == 2 and h == 1)
-        low_back = bank(7, [P, 2, V])
-        for t in range(2):
-            for h in range(2):
-                nc.tensor.transpose(low_back[:, t, halves[h]], low_turned[:, h, t, :], ident[:])
-        low_result = tile("low_result", [P, 2, V], F32)
-        nc.scalar.copy(out=low_result[:], in_=low_back[:])
-        nc.sync.dma_start(out=out_flat[:, 0 : 2 * V], in_=low_result[:].rearrange("p t v -> p (t v)"))
         turned3 = bank(6, [P, 2, P])
         for c in range(2):
             add_turned(turned3, weighted(3, c), c == 0, c == 1)
@@ -230,8 +223,15 @@ def tile_picked_bilin_none_lo_kernel(
         nc.scalar.copy(out=turned_sb[:], in_=turned3[:])
         for h in range(2):
             turn(back[1][:, halves[h]], turned_sb[:, h, :], h == 0, h == 1)
-        for h in range(2):
-            nc.scalar.copy(out=o_bf[h][:, :, 0:2], in_=low_result[:, :, halves[h]].rearrange("p t v -> p v t"))
+        low_back = bank(7, [P, 2, V])
+        for t in range(2):
+            for h in range(2):
+                nc.tensor.transpose(low_back[:, t, halves[h]], low_turned[:, h, t, :], ident[:])
+        low_result = tile("low_result", [P, 2, V], F32)
+        nc.scalar.copy(out=low_result[:], in_=low_back[:])
+        nc.sync.dma_start(out=out_flat[:, 0 : 2 * V], in_=low_result[:].rearrange("p t v -> p (t v)"))
+        for h, copy in enumerate((nc.scalar.copy, nc.vector.tensor_copy)):
+            copy(out=o_bf[h][:, :, 0:2], in_=low_result[:, :, halves[h]].rearrange("p t v -> p v t"))
         high_result = tile("high_result", [P, 2, V], F32)
         last3 = [weighted(3, c) for c in (2, 3)]
         last2 = weighted(2, 3)

@@ -66,12 +66,13 @@ def tile_picked_bilin_none_lo_kernel(
         nc.scalar.activation(sides[:, 0, :], f_turned[:, 0:4], COPY, bias=1.0, scale=-1.0)
         nc.scalar.copy(out=sides[:, 1, :], in_=f_turned[:, 0:4])
         weight_row = []
-        weight_keep = tile("weight_keep", [P, 4, 2], F32)
+        weight_keep = tile("weight_keep", [P, 3, 2], F32)
         for u in range(2):
             weight_col = tile(("pairs", "x_bf")[u], [P, 2, 2], F32)
             for h in range(2):
                 nc.scalar.activation(weight_col[:, :, h], sides[:, :, h], COPY, scale=sides[:, u, 2 + h : 3 + h])
-            nc.scalar.copy(out=weight_keep[:, 2 * u : 2 * u + 2, :], in_=weight_col[:])
+            kept = 2 - u
+            nc.scalar.copy(out=weight_keep[:, 2 * u : 2 * u + kept, :], in_=weight_col[:, 0:kept, :])
             spread = bank(6 + u, [P, 2, 2, P])
             for i in range(2):
                 for h in range(2):

@@ -66,13 +66,13 @@ def tile_picked_bilin_none_lo_kernel(
         nc.scalar.activation(sides[:, 0, :], f_turned[:, 0:4], COPY, bias=1.0, scale=-1.0)
         nc.scalar.copy(out=sides[:, 1, :], in_=f_turned[:, 0:4])
         weight_row = []
-        weight_keep = tile("weight_keep", [P, 3, 2], F32)
+        weight_keep = tile("weight_keep", [P, 2, 2], F32)
         for u in range(2):
             weight_col = tile(("pairs", "x_bf")[u], [P, 2, 2], F32)
             for h in range(2):
                 nc.scalar.activation(weight_col[:, :, h], sides[:, :, h], COPY, scale=sides[:, u, 2 + h : 3 + h])
-            kept = 2 - u
-            nc.scalar.copy(out=weight_keep[:, 2 * u : 2 * u + kept, :], in_=weight_col[:, 0:kept, :])
+            if u == 0:
+                nc.scalar.copy(out=weight_keep[:], in_=weight_col[:])
             spread = bank(6 + u, [P, 2, 2, P])
             for i in range(2):
                 for h in range(2):
@@ -199,49 +199,53 @@ def tile_picked_bilin_none_lo_kernel(
                 in_=turned[:].rearrange("v h (m t) -> v h t m", t=2),
             )
 
-        project(1)
         project(2)
-        turned0 = low_sum(0, 6)
-        spokes = [bank(c, [P, 2, P]) for c in range(3)]
-        for c in range(3):
-            add_turned(spokes[c], plain(2, c), True, True)
-            if c == 1:
-                low_copy(0, turned0)
         project(3)
-        turned1 = low_sum(1, 3)
+        project(1)
+        turned0 = low_sum(0, 6)
         back = [bank(4, [P, V]), bank(5, [P, V])]
-        for c in range(3):
-            if c == 2:
-                low_copy(1, turned1)
-            scaled = tile("scaled%d" % c, [P, 2, P], F32)
+
+        def spoke(c):
+            turned = bank(c, [P, 2, 2, P])
+            for i in range(2):
+                term = plain(2 + i, c)
+                for h in range(2):
+                    turn(turned[:, h, i, :], term[:, halves[h]], True, True)
+            return turned
+
+        def scale_back(c, turned):
+            scaled = tile("scaled%d" % c, [P, 2, 2, P], F32)
             for h in range(2):
-                nc.scalar.activation(scaled[:, h, :], spokes[c][:, h, :], COPY, scale=weight_keep[:, c, h : h + 1])
-                turn(back[0][:, halves[h]], scaled[:, h, :], c == 0 and h == 0, c == 2 and h == 1)
-        turned3 = bank(6, [P, 2, P])
-        for c in range(2):
-            add_turned(turned3, weighted(3, c), c == 0, c == 1)
-        turned_sb = tile("turned3", [P, 2, P], F32)
-        nc.scalar.copy(out=turned_sb[:], in_=turned3[:])
-        for h in range(2):
-            turn(back[1][:, halves[h]], turned_sb[:, h, :], h == 0, h == 1)
+                nc.scalar.activation(scaled[:, h, :, :], turned[:, h, :, :], COPY, scale=weight_keep[:, c, h : h + 1])
+                for i in range(2):
+                    turn(back[i][:, halves[h]], scaled[:, h, i, :], c == 0 and h == 0, c == 1 and h == 1)
+            return scaled
+
+        spoke0 = spoke(0)
+        low_copy(0, turned0)
+        turned1 = low_sum(1, 3)
+        scale_back(0, spoke0)
+        spoke1 = spoke(1)
+        low_copy(1, turned1)
         low_back = bank(7, [P, 2, V])
         for t in range(2):
             for h in range(2):
                 nc.tensor.transpose(low_back[:, t, halves[h]], low_turned[:, h, t, :], ident[:])
+        scaled = scale_back(1, spoke1)
         low_result = tile("low_result", [P, 2, V], F32)
         nc.scalar.copy(out=low_result[:], in_=low_back[:])
         nc.sync.dma_start(out=out_flat[:, 0 : 2 * V], in_=low_result[:].rearrange("p t v -> p (t v)"))
-        for h, copy in enumerate((nc.scalar.copy, nc.vector.tensor_copy)):
-            copy(out=o_bf[h][:, :, 0:2], in_=low_result[:, :, halves[h]].rearrange("p t v -> p v t"))
+        for h in range(2):
+            nc.scalar.copy(out=o_bf[h][:, :, 0:2], in_=low_result[:, :, halves[h]].rearrange("p t v -> p v t"))
         high_result = tile("high_result", [P, 2, V], F32)
-        last3 = [weighted(3, c) for c in (2, 3)]
-        last2 = weighted(2, 3)
-        pair3 = tile("pair3", [P, V], F32)
-        nc.vector.tensor_tensor(pair3[:], last3[0][:], last3[1][:], ADD)
-        nc.vector.tensor_tensor(high_result[:, 0, :], last2[:], back[0][:], ADD)
+        last = [[weighted(t, c) for t in (2, 3)] for c in (2, 3)]
+        pair = [tile("pair%d" % t, [P, V], F32) for t in (2, 3)]
+        for i in range(2):
+            nc.vector.tensor_tensor(pair[i][:], last[0][i][:], last[1][i][:], ADD)
+        nc.vector.tensor_tensor(high_result[:, 0, :], pair[0][:], back[0][:], ADD)
         nc.sync.dma_start(out=out_flat[:, 2 * V : 3 * V], in_=high_result[:, 0, :])
         for h in range(2):
-            nc.vector.tensor_tensor(high_result[:, 1, halves[h]], pair3[:, halves[h]], back[1][:, halves[h]], ADD)
+            nc.vector.tensor_tensor(high_result[:, 1, halves[h]], pair[1][:, halves[h]], back[1][:, halves[h]], ADD)
         nc.sync.dma_start(out=out_flat[:, 3 * V :], in_=high_result[:, 1, :])
 
         o_codes = tile("o_codes", [P, V], U32)
@@ -254,7 +258,7 @@ def tile_picked_bilin_none_lo_kernel(
             nc.sync.dma_start(out=word_rows[:, halves[h]], in_=o_codes[:, halves[h]].bitcast(I32))
         scale_rows = out_2[0].bitcast(I32)
         for q in range(4):
-            queue = nc.scalar if q % 2 == 0 else nc.sync
+            queue = nc.scalar if q == 0 else nc.sync
             queue.dma_start(
                 out=scale_rows[4 * q : 4 * q + 4, :], in_=o_scales[32 * q : 32 * q + 4, :].bitcast(I32)
             )

from contextlib import ExitStack

import concourse.mybir as mybir
from concourse.masks import make_identity

K, T, S, V, N = 512, 1024, 512, 256, 512
FLOPS = 2 * K * S * N

F32 = mybir.dt.float32
BF16 = mybir.dt.bfloat16
U32 = mybir.dt.uint32
I32 = mybir.dt.int32
U16 = mybir.dt.uint16
U8 = mybir.dt.uint8
FP8X4 = mybir.dt.float8_e4m3fn_x4
MULT = mybir.AluOpType.mult
ADD = mybir.AluOpType.add
COPY = mybir.ActivationFunctionType.Copy

P = 128
PACK = 4
HALF_S = S // 2
HALF_V = V // 2


def tile_picked_bilin_none_lo_kernel(
    tc, xT, w1, fx, fy, offs, c00, c01, c10, c11, out_0, out_1, out_2
):
    nc = tc.nc
    with ExitStack() as ctx:
        sb = ctx.enter_context(tc.tile_pool(name="sb", bufs=1))
        ps = ctx.enter_context(tc.psum_pool(name="ps", bufs=1))

        def tile(name, shape, dtype):
            return sb.tile(shape, dtype, name=name, align_bytes=64)

        def bank(number, shape):
            return ps.tile(shape, F32, name="bank%d" % number)

        x_rows = xT.rearrange("(p j) c -> p j c", j=PACK)
        w_rows = w1.rearrange("(p j) c -> p j c", j=PACK)
        x_plane = [tile("x_plane%d" % j, [P, T], F32) for j in range(PACK)]
        w_raw = [tile("w_raw%d" % u, [P, PACK, N // 2], F32) for u in range(2)]
        picked = sb.tile([P, S // 16], U16, name="picked")
        corner = [sb.tile([P, V // 16], U16, name="corner%d" % c) for c in range(4)]
        f_rows = tile("f_rows", [P, P], F32)
        nc.vector.memset(f_rows[:], 0.0)

        nc.sync.dma_start(out=x_plane[0][:], in_=x_rows[:, 0, :])
        nc.sync.dma_start(picked[:], offs)
        for a, f in enumerate((fx, fy)):
            nc.sync.dma_start(out=f_rows[2 * a : 2 * a + 2, :], in_=f[0:1, :].rearrange("o (h n) -> (o h) n", h=2))
        for j in range(1, PACK):
            nc.sync.dma_start(out=x_plane[j][:], in_=x_rows[:, j, :])
        for u in range(2):
            nc.sync.dma_start(out=w_raw[u][:], in_=w_rows[:, :, u * (N // 2) : (u + 1) * (N // 2)])
        for c, lst in enumerate((c00, c01, c10, c11)):
            nc.sync.dma_start(corner[c][:], lst)

        ident = tile("ident", [P, P], F32)
        make_identity(nc, ident[:])

        f_turned = bank(5, [P, P])
        nc.tensor.transpose(f_turned[:], f_rows[:], ident[:])
        sides = tile("sides", [P, 2, 4], F32)
        nc.scalar.activation(sides[:, 0, :], f_turned[:, 0:4], COPY, bias=1.0, scale=-1.0)
        nc.scalar.copy(out=sides[:, 1, :], in_=f_turned[:, 0:4])
        weight_row = []
        weight_keep = tile("weight_keep", [P, 2, 2], F32)
        for u in range(2):
            weight_col = tile(("pairs", "x_bf")[u], [P, 2, 2], F32)
            for h in range(2):
                nc.scalar.activation(weight_col[:, :, h], sides[:, :, h], COPY, scale=sides[:, u, 2 + h : 3 + h])
            if u == 0:
                nc.scalar.copy(out=weight_keep[:], in_=weight_col[:])
            spread = bank(6 + u, [P, 2, 2, P])
            for i in range(2):
                for h in range(2):
                    nc.tensor.transpose(spread[:, i, h, :], weight_col[:, i, h : h + 1].to_broadcast([P, P]), ident[:])
            rows = tile("weight_rows%d" % u, [P, 2, V], F32)
            nc.scalar.copy(out=rows[:].rearrange("p i v -> p (i v)"), in_=spread[:].rearrange("p i h n -> p (i h n)"))
            weight_row.extend([rows[:, 0, :], rows[:, 1, :]])

        x_codes = tile("x_codes", [P, S], U32)
        x_scales = tile("x_scales", [P, S], U8)
        pairs = tile("pairs", [P, 2, 2, HALF_S, 2], BF16)
        first_rows = tile("first_rows", [P, 2, S], BF16)
        for j in range(2):
            nc.vector.tensor_copy(first_rows[:, j, :], x_plane[j][:].indirect(picked[:]))
        nc.scalar.copy(out=pairs[:, :, 0, :, :], in_=first_rows[:].rearrange("p e (h s) -> p h s e", h=2))
        nc.vector.tensor_copy(pairs[:, :, 1, :, 0], x_plane[2][:].indirect(picked[:]))
        for h in range(2):
            nc.vector.tensor_copy(
                pairs[:, h, 1, :, 1],
                x_plane[3][:].indirect(picked[:, h * (HALF_S // 16) : (h + 1) * (HALF_S // 16)]),
            )
        pieces = ((0, HALF_S), (HALF_S, HALF_S + P), (HALF_S + P, S))
        x_bf = tile("x_bf", [P, S * PACK], BF16)
        for lo, hi in pieces:
            words = pairs[:, lo // HALF_S, :, :, :].rearrange("p u s e -> p (u s e)").bitcast(U32)
            first = lo % HALF_S // 2
            nc.scalar.copy(
                out=x_bf[:, lo * PACK : hi * PACK].bitcast(U32).rearrange("p (c i u) -> p c u i", i=2, u=2),
                in_=words.rearrange("p (u c i) -> p c u i", u=2, i=2)[:, first : first + (hi - lo) // 2, :, :],
            )

        def quantize(codes, scales, values):
            nc.vector.quantize_mx(out=codes.bitcast(FP8X4), scales=scales, in_=values)

        def quantize_x(i):
            lo, hi = pieces[i]
            quantize(x_codes[:, lo:hi], x_scales[:, lo:hi], x_bf[:, lo * PACK : hi * PACK])

        def product(acc, codes, scales, cols):
            nc.tensor.matmul_mx(
                out=acc,
                lhsT=codes.bitcast(FP8X4),
                lhsT_scale=scales,
                rhs=x_codes[:, cols].bitcast(FP8X4),
                rhs_scale=x_scales[:, cols],
                start=True,
                stop=True,
            )

        w_view = [raw[:].rearrange("p j (m t) -> p m j t", t=PACK) for raw in w_raw]
        y = [tile("y0", [P, S], F32)]
        low_codes = [tile("low_codes%d" % u, [P, P], U32) for u in range(2)]
        low_scales = [tile("low_scales%d" % u, [P, P], U8) for u in range(2)]

        dealt_first = tile("x_plane2", [P, P // 2, 2, PACK], BF16)
        nc.vector.tensor_copy(out=dealt_first[:].rearrange("p m t j -> p m j t"), in_=w_view[0][:, :, :, 0:2])
        quantize_x(0)
        quantize(low_codes[0][:], low_scales[0][:], dealt_first[:].rearrange("p m t j -> p (m t j)"))
        quantize_x(1)
        quantize_x(2)

        dealt_scalar = tile("first_rows", [P, 2, P // 2, PACK], BF16)
        nc.scalar.copy(out=dealt_scalar[:].rearrange("p t m j -> p m j t"), in_=w_view[0][:, :, :, 2:4])
        for i, (lo, hi) in enumerate((lo, lo + P) for lo in range(0, S, P)):
            acc = bank(i, [P, hi - lo])
            product(acc[:], low_codes[0][:], low_scales[0][:], slice(lo, hi))
            nc.scalar.copy(out=y[0][:, lo:hi], in_=acc[:])
        dealt_vector = tile("pairs", [P, 2, P * PACK], BF16)
        dealt_high = dealt_vector[:, 1, :].rearrange("p (t m j) -> p t m j", t=2, j=PACK)
        nc.vector.tensor_copy(
            out=dealt_vector[:, 0, :].rearrange("p (m t j) -> p m j t", t=2, j=PACK), in_=w_view[1][:, :, :, 0:2]
        )
        nc.vector.tensor_copy(out=dealt_high.rearrange("p t m j -> p m j t"), in_=w_view[1][:, :, :, 2:4])
        quantize(low_codes[1][:], low_scales[1][:], dealt_vector[:, 0, :])
        high_codes = tile("high_codes", [P, 2 * P], U32)
        high_scales = tile("high_scales", [P, 2 * P], U8)
        for u, dealt in enumerate((dealt_scalar[:], dealt_high)):
            for t in range(2):
                cols = slice(t * P + u * (P // 2), t * P + (u + 1) * (P // 2))
                quantize(high_codes[:, cols], high_scales[:, cols], dealt[:, t, :, :].rearrange("p m j -> p (m j)"))
        y.extend([tile(name, [P, S], F32) for name in ("y1", "y2", "y3")])

        def project(t):
            acc = bank((None, 7, 4, 5)[t], [P, S])
            if t == 1:
                product(acc[:], low_codes[1][:], low_scales[1][:], slice(0, S))
            else:
                cols = slice((t - 2) * P, (t - 1) * P)
                product(acc[:], high_codes[:, cols], high_scales[:, cols], slice(0, S))
            nc.scalar.copy(out=y[t][:], in_=acc[:])

        halves = [slice(h * HALF_V, (h + 1) * HALF_V) for h in range(2)]

        def weighted(t, c):
            term = tile("term%d_%d" % (t, c), [P, V], F32)
            nc.vector.tensor_tensor(term[:], y[t][:].indirect(corner[c][:]), weight_row[c], MULT)
            return term

        def plain(t, c):
            term = tile("term%d_%d" % (t, c), [P, V], F32)
            nc.scalar.activation(term[:], y[t][:].indirect(corner[c][:]), COPY)
            return term

        def turn(out, in_, start, stop):
            nc.tensor.matmul(out, lhsT=in_, rhs=ident[:], is_transpose=True, start=start, stop=stop)

        def add_turned(turned, term, first, last):
            for h in range(2):
                turn(turned[:, h, :], term[:, halves[h]], first and h == 0, last and h == 1)

        out_flat = out_0.rearrange("(p t) v -> p (t v)", t=PACK)
        o_bf = [tile("o_bf%d" % h, [P, HALF_V, PACK], BF16) for h in range(2)]
        low_turned = tile("low_turned", [P, 2, 2, P], F32)

        def low_sum(u, number):
            turned = bank(number, [P, 2, P])
            for c in range(4):
                add_turned(turned, weighted(u, c), c == 0, c == 3)
            return turned

        def low_copy(u, turned):
            nc.scalar.copy(
                out=low_turned[:, :, :, u * (P // 2) : (u + 1) * (P // 2)],
                in_=turned[:].rearrange("v h (m t) -> v h t m", t=2),
            )

        project(2)
        project(3)
        project(1)
        turned0 = low_sum(0, 6)
        back = [bank(4, [P, V]), bank(5, [P, V])]

        def spoke(c):
            turned = bank(c, [P, 2, 2, P])
            for i in range(2):
                term = plain(2 + i, c)
                for h in range(2):
                    turn(turned[:, h, i, :], term[:, halves[h]], True, True)
            return turned

        def scale_back(c, turned):
            scaled = tile("scaled%d" % c, [P, 2, 2, P], F32)
            for h in range(2):
                nc.scalar.activation(scaled[:, h, :, :], turned[:, h, :, :], COPY, scale=weight_keep[:, c, h : h + 1])
                for i in range(2):
                    turn(back[i][:, halves[h]], scaled[:, h, i, :], c == 0 and h == 0, c == 1 and h == 1)
            return scaled

        spoke0 = spoke(0)
        low_copy(0, turned0)
        turned1 = low_sum(1, 3)
        scale_back(0, spoke0)
        spoke1 = spoke(1)
        low_copy(1, turned1)
        low_back = bank(7, [P, 2, V])
        for t in range(2):
            for h in range(2):
                nc.tensor.transpose(low_back[:, t, halves[h]], low_turned[:, h, t, :], ident[:])
        scaled = scale_back(1, spoke1)
        low_result = tile("low_result", [P, 2, V], F32)
        nc.scalar.copy(out=low_result[:], in_=low_back[:])
        nc.sync.dma_start(out=out_flat[:, 0 : 2 * V], in_=low_result[:].rearrange("p t v -> p (t v)"))
        for h in range(2):
            nc.scalar.copy(out=o_bf[h][:, :, 0:2], in_=low_result[:, :, halves[h]].rearrange("p t v -> p v t"))
        high_result = tile("high_result", [P, 2, V], F32)
        last = [[weighted(t, c) for t in (2, 3)] for c in (2, 3)]
        pair = [tile("pair%d" % t, [P, V], F32) for t in (2, 3)]
        for i in range(2):
            nc.vector.tensor_tensor(pair[i][:], last[0][i][:], last[1][i][:], ADD)
        nc.vector.tensor_tensor(high_result[:, 0, :], pair[0][:], back[0][:], ADD)
        nc.sync.dma_start(out=out_flat[:, 2 * V : 3 * V], in_=high_result[:, 0, :])
        for h in range(2):
            nc.vector.tensor_tensor(high_result[:, 1, halves[h]], pair[1][:, halves[h]], back[1][:, halves[h]], ADD)
        nc.sync.dma_start(out=out_flat[:, 3 * V :], in_=high_result[:, 1, :])

        o_codes = tile("o_codes", [P, V], U32)
        o_scales = tile("o_scales", [P, V], U8)
        word_rows = out_1[0].rearrange("l c r -> l (c r)").bitcast(I32)
        for h in range(2):
            nc.vector.tensor_copy(out=o_bf[h][:, :, 2:4], in_=high_result[:, :, halves[h]].rearrange("p t v -> p v t"))
        for h in range(2):
            quantize(o_codes[:, halves[h]], o_scales[:, halves[h]], o_bf[h][:].rearrange("p v t -> p (v t)"))
            nc.sync.dma_start(out=word_rows[:, halves[h]], in_=o_codes[:, halves[h]].bitcast(I32))
        scale_rows = out_2[0].bitcast(I32)
        for q in range(4):
            queue = nc.scalar if q == 0 else nc.sync
            queue.dma_start(
                out=scale_rows[4 * q : 4 * q + 4, :], in_=o_scales[32 * q : 32 * q + 4, :].bitcast(I32)
            )
